import numpy as np, ml_dtypes
CORES = [3,5,19,21,35,37,51,53,67,69]
N = 10
S, B = 2, 128
NT = N * S
def setup_inputs(rng):
    a = (rng.standard_normal((128, 128), dtype=np.float32) / 12).astype(ml_dtypes.bfloat16)
    return {"x": rng.standard_normal((N, 128, S * B), dtype=np.float32).astype(ml_dtypes.bfloat16), "a": np.broadcast_to(a, (N, 128, 128)).copy(), "at": np.broadcast_to(a.T, (N, 128, 128)).copy()}
def setup_inputs_big(rng):
    d = setup_inputs(rng)
    for k in ("x",): d[k] = (d[k].astype(np.float32) * 1048576.0).astype(d[k].dtype)
    return d
def setup_inputs_small(rng):
    d = setup_inputs(rng)
    for k in ("x",): d[k] = (d[k].astype(np.float32) * (1 / 1048576.0)).astype(d[k].dtype)
    return d
def setup_inputs_apart(rng):
    d = setup_inputs(rng)
    f = (10.0 ** rng.permutation(np.linspace(-1.5, 1.5, N))).astype(np.float32).reshape(N, 1, 1)
    for k in ("x",): d[k] = (d[k].astype(np.float32) * f).astype(d[k].dtype)
    return d
def reference(x, a, at):
    A = a[0].astype(np.float64); X = [x[t // S][:, B * (t % S):B * (t % S) + B].astype(np.float64) for t in range(NT)]
    f = [None] * NT; b = [None] * NT; h = np.zeros((128, B))
    for t in range(NT):
        h = A.T @ h + X[t]; f[t] = h
    h = np.zeros((128, B))
    for t in range(NT - 1, -1, -1):
        h = A.T @ h + X[t]; b[t] = h
    return {"y": np.stack([np.concatenate([f[r * S + s] + b[r * S + s] for s in range(S)], axis=1) for r in range(N)]).astype(ml_dtypes.bfloat16)}

@@ -1,0 +1,192 @@
+from concourse.bass import DstId, RemoteDMATransfer
+from concourse.mybir import AluOpType
+
+B = 128
+
+SCRATCH = {
+    "X4": ("sbuf", [128, 4 * B], "bfloat16"),
+    "X2": ("sbuf", [128, 2 * B], "bfloat16"),
+    "AT": ("sbuf", [128, B], "bfloat16"),
+    "W": ("sbuf", [128, 14 * B], "bfloat16"),
+    "CD": ("sbuf", [128, 2 * B], "bfloat16"),
+    "RC": ("sbuf", [128, 4 * B], "bfloat16"),
+    "Y": ("sbuf", [128, 2 * B], "bfloat16"),
+    "PA": ("psum", [128, 512], "float32"),
+    "PB": ("psum", [128, 512], "float32"),
+    "PC": ("psum", [128, 512], "float32"),
+    "PD": ("psum", [128, 512], "float32"),
+    "PY0": ("psum", [128, 512], "float32"),
+    "PY1": ("psum", [128, 512], "float32"),
+}
+SEMAPHORES = ["lx", "la", "lat", "xp", "ls", "s1", "e1", "s2", "e2", "s3", "e3", "s4", "e4", "sC", "sD", "ecd", "ex2",
+              "sY0", "sY1", "ey", "st", "r0", "r1", "r2", "r3"]
+
+
+def _bits(mask):
+    return [1 << i for i in range(mask.bit_length()) if (mask >> i) & 1]
+
+
+def rank_program(g, core, T, topo):
+    if T.rank_of(core) is None:
+        return
+    S = T.sem
+    te, ve = g.tensor, g.vector
+
+    cores = list(T.cores)
+    chips = []
+    for c in cores:
+        if topo.chip(c) not in chips:
+            chips.append(topo.chip(c))
+    groups = [[c for c in cores if topo.chip(c) == ch] for ch in chips]
+    nch = len(chips)
+    k = chips.index(topo.chip(core))
+    role = groups[k].index(core)
+    partner = groups[k][1 - role]
+    peer = {}
+    for j in range(nch):
+        if j != k:
+            peer[j] = [c for c in groups[j] if topo.die(c) == topo.die(core)][0]
+            assert topo.may_write(core, peer[j])
+    m = topo.mask(core, partner)
+    for j in peer:
+        m &= topo.mask(core, peer[j])
+    eng = _bits(m)
+    per = len(eng) // (nch - 1)
+    n1 = len(eng)
+
+    def xb(v):
+        return T.X4[:, v * B:(v + 1) * B]
+
+    own = (2 * role, 2 * role + 1)
+    oth = (2 - 2 * role, 3 - 2 * role)
+    need_c, need_d = k < nch - 1, k > 0
+
+    g.sync.dma_start(T.X4[:, own[0] * B:(own[1] + 1) * B], T.x[:, :]).then_inc(S.lx, 16)
+    g.scalar.dma_start(T.W[:, 0:B], T.a[:, :]).then_inc(S.la, 16)
+    g.sync.dma_start(T.AT[:, :], T.at[:, :]).then_inc(S.lat, 16)
+
+    rid, pid, _se = topo.addr(partner)
+    g.wait_ge(S.lx, 16)
+    g.remote_dma(out_ap=T.X4[:, own[0] * B:(own[1] + 1) * B], in_ap=T.X4[:, own[0] * B:(own[1] + 1) * B],
+                 remote_sem=S.xp, local_sem=S.ls, pid=pid, routing_id=rid, dma_engine_mask=m)
+
+    pa = {1: 0, 2: B, 3: 3 * B, 4: 4 * B}
+    pt = {2: 2 * B, 4: 5 * B}
+
+    def A(p, n=1):
+        return T.W[:, pa[p]:pa[p] + n * B]
+
+    def At(q):
+        return T.W[:, pt[q]:pt[q] + B]
+
+    te.wait_ge(S.la, 16)
+    te.wait_ge(S.lat, 16)
+    te.matmul(T.PA[:, 0:B], T.AT[:, :], A(1), start=True, stop=True).then_inc(S.s1, 1)
+    te.matmul(T.PA[:, B:2 * B], A(1), T.AT[:, :], start=True, stop=True).then_inc(S.s1, 1)
+    ve.wait_ge(S.s1, 2)
+    ve.tensor_copy(T.W[:, B:3 * B], T.PA[:, 0:2 * B]).then_inc(S.e1, 1)
+    te.wait_ge(S.e1, 1)
+    te.matmul(T.PB[:, 0:2 * B], At(2), A(1, 2), start=True, stop=True).then_inc(S.s2, 1)
+    te.matmul(T.PB[:, 2 * B:3 * B], A(2), At(2), start=True, stop=True).then_inc(S.s2, 1)
+    ve.wait_ge(S.s2, 2)
+    ve.tensor_copy(T.W[:, 3 * B:6 * B], T.PB[:, 0:3 * B]).then_inc(S.e2, 1)
+    te.wait_ge(S.e2, 1)
+    te.wait_ge(S.lx, 16)
+
+    jobs = []
+    if need_c:
+        jobs.append((T.PC, S.sC, [(3, 0), (2, 1), (1, 2)], 3, 0))
+    if need_d:
+        jobs.append((T.PD, S.sD, [(1, 1), (2, 2), (3, 3)], 0, 1))
+    jobs.sort(key=lambda jb: len([1 for (_p, v) in jb[2] if v in oth]))
+    for (ps, sem, terms, _plain, _slot) in jobs:
+        mine = [t for t in terms if t[1] in own]
+        for i, (p, v) in enumerate(mine):
+            te.matmul(ps[:, 0:B], A(p), xb(v), start=(i == 0), stop=False).then_inc(sem, 1)
+    te.wait_ge(S.xp, n1)
+    ve.wait_ge(S.xp, n1)
+    ve.wait_ge(S.lx, 16)
+    for (ps, sem, terms, plain, slot) in jobs:
+        theirs = [t for t in terms if t[1] in oth]
+        for i, (p, v) in enumerate(theirs):
+            te.matmul(ps[:, 0:B], A(p), xb(v), start=False, stop=(i == len(theirs) - 1)).then_inc(sem, 1)
+        ve.wait_ge(sem, len(terms))
+        ve.tensor_tensor(T.CD[:, slot * B:(slot + 1) * B], ps[:, 0:B], xb(plain), AluOpType.add).then_inc(S.ecd, 1)
+
+    g.wait_ge(S.ecd, len(jobs))
+    trs = []
+    for i, j in enumerate(sorted(peer)):
+        rid, pid, _se = topo.addr(peer[j])
+        slot = 0 if j > k else 1
+        land = k if k < j else k - 1
+        mk = 0
+        for b in eng[i * per:(i + 1) * per]:
+            mk |= b
+        trs.append(RemoteDMATransfer(dst_ids=[DstId(rid=rid, pnc=pid)], dma_engine_mask=mk,
+                                     remote_sem=S["r%d" % land], src=T.CD[:, slot * B:(slot + 1) * B],
+                                     dst=T.RC[:, land * B:(land + 1) * B]))
+    g.remote_dma_fused(trs, local_sem=S.ls)
+
+    ve.tensor_tensor(T.X2[:, :], T.X4[:, own[0] * B:(own[1] + 1) * B], T.X4[:, own[0] * B:(own[1] + 1) * B],
+                     AluOpType.add).then_inc(S.ex2, 1)
+    nfw, nbw = k, nch - 1 - k
+    levels = {1: (nfw if role == 0 else nbw), 3: (nbw if role == 0 else nfw)}
+    col = 6 * B
+    off, n3 = 0, 0
+    for h in (1, 3):
+        if levels[h] >= 2:
+            te.matmul(T.PA[:, off:off + 2 * B], At(4), A(h, 2), start=True, stop=True).then_inc(S.s3, 1)
+            pa[h + 4], pa[h + 5] = col + off, col + off + B
+            off += 2 * B
+            n3 += 1
+    if max(levels.values()) >= 3:
+        te.matmul(T.PA[:, off:off + B], A(4), At(4), start=True, stop=True).then_inc(S.s3, 1)
+        pt[8] = col + off
+        off += B
+        n3 += 1
+    if n3:
+        ve.wait_ge(S.s3, n3)
+        ve.tensor_copy(T.W[:, col:col + off], T.PA[:, 0:off]).then_inc(S.e3, 1)
+        col += off
+    py, sy, ny = (T.PY0, T.PY1), (S.sY0, S.sY1), [0, 0]
+    for s in (0, 1):
+        u = own[s]
+        for v in range(4):
+            if v != u:
+                te.matmul(py[s][:, 0:B], A(abs(u - v)), xb(v), start=(ny[s] == 0), stop=False).then_inc(sy[s], 1)
+                ny[s] += 1
+    if n3:
+        te.wait_ge(S.e3, 1)
+    off, n4 = 0, 0
+    for h in (1, 3):
+        for lv in (2, 3):
+            if levels[h] > lv:
+                te.matmul(T.PB[:, off:off + 2 * B], At(8), A(h + 4 * (lv - 2), 2), start=True, stop=True).then_inc(S.s4, 1)
+                pa[h + 4 * lv], pa[h + 4 * lv + 1] = col + off, col + off + B
+                off += 2 * B
+                n4 += 1
+    if n4:
+        ve.wait_ge(S.s4, n4)
+        ve.tensor_copy(T.W[:, col:col + off], T.PB[:, 0:off]).then_inc(S.e4, 1)
+        te.wait_ge(S.e4, 1)
+
+    order = sorted(peer, key=lambda j: -abs(2 * j - (nch - 1)))
+    for i, j in enumerate(order):
+        land = j if j < k else j - 1
+        te.wait_ge(S["r%d" % land], per)
+        for s in (0, 1):
+            u = own[s]
+            p = u + 1 + 4 * (k - 1 - j) if j < k else 4 - u + 4 * (j - k - 1)
+            te.matmul(py[s][:, 0:B], A(p), T.RC[:, land * B:(land + 1) * B], start=False,
+                      stop=(i == len(order) - 1)).then_inc(sy[s], 1)
+            ny[s] += 1
+
+    ve.wait_ge(S.ex2, 1)
+    for s in (0, 1):
+        ve.wait_ge(sy[s], ny[s])
+        ve.tensor_tensor(T.Y[:, s * B:(s + 1) * B], py[s][:, 0:B], T.X2[:, s * B:(s + 1) * B],
+                         AluOpType.add).then_inc(S.ey, 1)
+    g.sync.wait_ge(S.ey, 2)
+    g.sync.dma_start(T.y[:, :], T.Y[:, :]).then_inc(S.st, 16)
+    g.sync.wait_ge(S.st, 16)
+    g.wait_ge(S.ls, n1 + per * len(trs))

@@ -7,23 +7,31 @@ SCRATCH = {
     "X4": ("sbuf", [128, 4 * B], "bfloat16"),
     "X2": ("sbuf", [128, 2 * B], "bfloat16"),
     "AT": ("sbuf", [128, B], "bfloat16"),
-    "W": ("sbuf", [128, 14 * B], "bfloat16"),
+    "W": ("sbuf", [128, 13 * B], "bfloat16"),
+    "PT": ("sbuf", [128, 2 * B], "bfloat16"),
     "CD": ("sbuf", [128, 2 * B], "bfloat16"),
-    "RC": ("sbuf", [128, 4 * B], "bfloat16"),
+    "RC": ("sbuf", [128, 5 * B], "bfloat16"),
     "Y": ("sbuf", [128, 2 * B], "bfloat16"),
     "PA": ("psum", [128, 512], "float32"),
     "PB": ("psum", [128, 512], "float32"),
+    "PE": ("psum", [128, 512], "float32"),
+    "PF": ("psum", [128, 512], "float32"),
     "PC": ("psum", [128, 512], "float32"),
     "PD": ("psum", [128, 512], "float32"),
     "PY0": ("psum", [128, 512], "float32"),
     "PY1": ("psum", [128, 512], "float32"),
 }
-SEMAPHORES = ["lx", "la", "lat", "xp", "ls", "s1", "e1", "s2", "e2", "s3", "e3", "s4", "e4", "sC", "sD", "ecd", "ex2",
-              "sY0", "sY1", "ey", "st", "r0", "r1", "r2", "r3"]
+SEMAPHORES = ["lx", "la", "lat", "xp", "ls", "sa2", "ea2", "st2", "et2", "sa3", "ea3", "sa4", "ea4", "st8", "et8",
+              "sP", "eP", "sQ", "eQ", "sL0", "sL1", "sL2", "eL0", "eL1", "eL2", "sC", "sD", "eC", "eD", "ex2",
+              "sY0", "sY1", "ey", "st", "r0", "r1", "r2", "r3", "r4"]
 
 
-def _bits(mask):
-    return [1 << i for i in range(mask.bit_length()) if (mask >> i) & 1]
+def _early(kk, nch):
+    return (kk + 1) % nch
+
+
+def _late_order(kk, rr, nch):
+    return [j for j in [(kk + (1 + s) * (1 - 2 * rr)) % nch for s in range(nch - 1)] if j != _early(kk, nch)]
 
 
 def rank_program(g, core, T, topo):
@@ -42,36 +50,45 @@ def rank_program(g, core, T, topo):
     k = chips.index(topo.chip(core))
     role = groups[k].index(core)
     partner = groups[k][1 - role]
-    peer = {}
-    for j in range(nch):
-        if j != k:
-            peer[j] = [c for c in groups[j] if topo.die(c) == topo.die(core)][0]
-            assert topo.may_write(core, peer[j])
+    others = [j for j in range(nch) if j != k]
+    peer = {j: [c for c in groups[j] if topo.die(c) == topo.die(core)][0] for j in others}
     m = topo.mask(core, partner)
-    for j in peer:
-        m &= topo.mask(core, peer[j])
-    eng = _bits(m)
-    per = len(eng) // (nch - 1)
-    n1 = len(eng)
+    for j in others:
+        for c in groups[j]:
+            assert topo.may_write(core, c)
+            m &= topo.mask(core, c)
+    n1 = sum((m >> i) & 1 for i in range(m.bit_length()))
 
     def xb(v):
         return T.X4[:, v * B:(v + 1) * B]
 
+    def slot_of(src_chip, dst_chip):
+        return src_chip if src_chip < dst_chip else src_chip - 1
+
     own = (2 * role, 2 * role + 1)
     oth = (2 - 2 * role, 3 - 2 * role)
-    need_c, need_d = k < nch - 1, k > 0
+    xown = T.X4[:, own[0] * B:(own[1] + 1) * B]
+    je = _early(k, nch)
+    qe = 0 if je > k else 1
+    squared = qe == role
+    mylate = _late_order(k, role, nch)
+    need_c, need_d = any(j > k for j in mylate), any(j < k for j in mylate)
+    nfw, nbw = k, nch - 1 - k
+    hfw, hbw = (1, 3) if role == 0 else (3, 1)
+    levels = {hfw: nfw, hbw: nbw}
+    need8 = max(levels.values()) >= 3
 
-    g.sync.dma_start(T.X4[:, own[0] * B:(own[1] + 1) * B], T.x[:, :]).then_inc(S.lx, 16)
+    g.sync.dma_start(xown, T.x[:, :]).then_inc(S.lx, 16)
     g.scalar.dma_start(T.W[:, 0:B], T.a[:, :]).then_inc(S.la, 16)
     g.sync.dma_start(T.AT[:, :], T.at[:, :]).then_inc(S.lat, 16)
 
     rid, pid, _se = topo.addr(partner)
     g.wait_ge(S.lx, 16)
-    g.remote_dma(out_ap=T.X4[:, own[0] * B:(own[1] + 1) * B], in_ap=T.X4[:, own[0] * B:(own[1] + 1) * B],
-                 remote_sem=S.xp, local_sem=S.ls, pid=pid, routing_id=rid, dma_engine_mask=m)
+    g.remote_dma(out_ap=xown, in_ap=xown, remote_sem=S.xp, local_sem=S.ls, pid=pid, routing_id=rid, dma_engine_mask=m)
+    nls = n1
 
     pa = {1: 0, 2: B, 3: 3 * B, 4: 4 * B}
-    pt = {2: 2 * B, 4: 5 * B}
+    pt = {2: 2 * B, 4: 5 * B, 8: 6 * B}
 
     def A(p, n=1):
         return T.W[:, pa[p]:pa[p] + n * B]
@@ -81,104 +98,140 @@ def rank_program(g, core, T, topo):
 
     te.wait_ge(S.la, 16)
     te.wait_ge(S.lat, 16)
-    te.matmul(T.PA[:, 0:B], T.AT[:, :], A(1), start=True, stop=True).then_inc(S.s1, 1)
-    te.matmul(T.PA[:, B:2 * B], A(1), T.AT[:, :], start=True, stop=True).then_inc(S.s1, 1)
-    ve.wait_ge(S.s1, 2)
-    ve.tensor_copy(T.W[:, B:3 * B], T.PA[:, 0:2 * B]).then_inc(S.e1, 1)
-    te.wait_ge(S.e1, 1)
-    te.matmul(T.PB[:, 0:2 * B], At(2), A(1, 2), start=True, stop=True).then_inc(S.s2, 1)
-    te.matmul(T.PB[:, 2 * B:3 * B], A(2), At(2), start=True, stop=True).then_inc(S.s2, 1)
-    ve.wait_ge(S.s2, 2)
-    ve.tensor_copy(T.W[:, 3 * B:6 * B], T.PB[:, 0:3 * B]).then_inc(S.e2, 1)
-    te.wait_ge(S.e2, 1)
+    te.matmul(T.PA[:, 0:B], T.AT[:, :], A(1), start=True, stop=True).then_inc(S.sa2, 1)
+    te.matmul(T.PB[:, 0:B], A(1), T.AT[:, :], start=True, stop=True).then_inc(S.st2, 1)
+    ve.wait_ge(S.sa2, 1)
+    ve.tensor_copy(A(2), T.PA[:, 0:B]).then_inc(S.ea2, 1)
+    ve.wait_ge(S.st2, 1)
+    ve.tensor_copy(At(2), T.PB[:, 0:B]).then_inc(S.et2, 1)
+    te.wait_ge(S.ea2, 1)
     te.wait_ge(S.lx, 16)
+    ve.wait_ge(S.lx, 16)
+    te.matmul(T.PA[:, 0:B], A(1), xb(own[qe]), start=True, stop=True).then_inc(S.sP, 1)
+    te.matmul(T.PE[:, 0:B], T.AT[:, :], A(2), start=True, stop=True).then_inc(S.sa3, 1)
+    ve.wait_ge(S.sP, 1)
+    ve.tensor_tensor(T.PT[:, 0:B], T.PA[:, 0:B], xb(own[1 - qe]), AluOpType.add).then_inc(S.eP, 1)
+    ve.wait_ge(S.sa3, 1)
+    ve.tensor_copy(A(3), T.PE[:, 0:B]).then_inc(S.ea3, 1)
+    te.wait_ge(S.eP, 1)
+    if squared:
+        te.matmul(T.PA[:, 0:B], A(2), T.PT[:, 0:B], start=True, stop=True).then_inc(S.sQ, 1)
+        ve.wait_ge(S.sQ, 1)
+        ve.tensor_copy(T.PT[:, B:2 * B], T.PA[:, 0:B]).then_inc(S.eQ, 1)
+    te.wait_ge(S.et2, 1)
+    te.matmul(T.PF[:, 0:B], At(2), A(2), start=True, stop=True).then_inc(S.sa4, 1)
+    te.matmul(T.PF[:, B:2 * B], A(2), At(2), start=True, stop=True).then_inc(S.sa4, 1)
+    ve.wait_ge(S.sa4, 2)
+    ve.tensor_copy(T.W[:, 4 * B:6 * B], T.PF[:, 0:2 * B]).then_inc(S.ea4, 1)
 
+    g.wait_ge(S.eP, 1)
+    if squared:
+        g.wait_ge(S.eQ, 1)
+    land = slot_of(k, je) if role == 0 else nch - 1
+    ids = []
+    for c in groups[je]:
+        rid, pid, _se = topo.addr(c)
+        ids.append(DstId(rid=rid, pnc=pid))
+    g.remote_dma_fused([RemoteDMATransfer(dst_ids=ids, dma_engine_mask=m, remote_sem=S["r%d" % land],
+                                          srcs=[T.PT[:, B:2 * B] if squared else T.PT[:, 0:B]],
+                                          dsts=[T.RC[:, land * B:(land + 1) * B] for _c in ids])],
+                       local_sem=S.ls)
+    nls += n1
+
+    te.wait_ge(S.ea3, 1)
     jobs = []
     if need_c:
-        jobs.append((T.PC, S.sC, [(3, 0), (2, 1), (1, 2)], 3, 0))
+        jobs.append((T.PC, S.sC, [(3, 0), (2, 1), (1, 2)], 3, 0, S.eC))
     if need_d:
-        jobs.append((T.PD, S.sD, [(1, 1), (2, 2), (3, 3)], 0, 1))
+        jobs.append((T.PD, S.sD, [(1, 1), (2, 2), (3, 3)], 0, 1, S.eD))
     jobs.sort(key=lambda jb: len([1 for (_p, v) in jb[2] if v in oth]))
-    for (ps, sem, terms, _plain, _slot) in jobs:
+    for (ps, sem, terms, _plain, _q, _done) in jobs:
         mine = [t for t in terms if t[1] in own]
         for i, (p, v) in enumerate(mine):
             te.matmul(ps[:, 0:B], A(p), xb(v), start=(i == 0), stop=False).then_inc(sem, 1)
+    py, sy, ny = (T.PY0, T.PY1), (S.sY0, S.sY1), [0, 0]
+    for s in (0, 1):
+        te.matmul(py[s][:, 0:B], A(1), xb(own[1 - s]), start=True, stop=False).then_inc(sy[s], 1)
+        ny[s] += 1
+
     te.wait_ge(S.xp, n1)
     ve.wait_ge(S.xp, n1)
-    ve.wait_ge(S.lx, 16)
-    for (ps, sem, terms, plain, slot) in jobs:
+    for (ps, sem, terms, plain, q, done) in jobs:
         theirs = [t for t in terms if t[1] in oth]
         for i, (p, v) in enumerate(theirs):
             te.matmul(ps[:, 0:B], A(p), xb(v), start=False, stop=(i == len(theirs) - 1)).then_inc(sem, 1)
         ve.wait_ge(sem, len(terms))
-        ve.tensor_tensor(T.CD[:, slot * B:(slot + 1) * B], ps[:, 0:B], xb(plain), AluOpType.add).then_inc(S.ecd, 1)
+        ve.tensor_tensor(T.CD[:, q * B:(q + 1) * B], ps[:, 0:B], xb(plain), AluOpType.add).then_inc(done, 1)
+        dests = [j for j in mylate if (j > k) == (q == 0)]
+        land = k if q == 0 else k - 1
+        ids = []
+        for j in dests:
+            rid, pid, _se = topo.addr(peer[j])
+            ids.append(DstId(rid=rid, pnc=pid))
+        g.wait_ge(done, 1)
+        g.remote_dma_fused([RemoteDMATransfer(dst_ids=ids, dma_engine_mask=m, remote_sem=S["r%d" % land],
+                                              srcs=[T.CD[:, q * B:(q + 1) * B]],
+                                              dsts=[T.RC[:, land * B:(land + 1) * B] for _j in dests])],
+                           local_sem=S.ls)
+        nls += n1
 
-    g.wait_ge(S.ecd, len(jobs))
-    trs = []
-    for i, j in enumerate(sorted(peer)):
-        rid, pid, _se = topo.addr(peer[j])
-        slot = 0 if j > k else 1
-        land = k if k < j else k - 1
-        mk = 0
-        for b in eng[i * per:(i + 1) * per]:
-            mk |= b
-        trs.append(RemoteDMATransfer(dst_ids=[DstId(rid=rid, pnc=pid)], dma_engine_mask=mk,
-                                     remote_sem=S["r%d" % land], src=T.CD[:, slot * B:(slot + 1) * B],
-                                     dst=T.RC[:, land * B:(land + 1) * B]))
-    g.remote_dma_fused(trs, local_sem=S.ls)
+    te.wait_ge(S.ea4, 1)
+    if squared:
+        te.wait_ge(S.eQ, 1)
+    if need8:
+        te.matmul(T.PA[:, 0:B], A(4), At(4), start=True, stop=True).then_inc(S.st8, 1)
+        ve.wait_ge(S.st8, 1)
+        ve.tensor_copy(At(8), T.PA[:, 0:B]).then_inc(S.et8, 1)
+    pairs = [(h, lv) for lv in (1, 2, 3) for h in (1, 3) if levels[h] > lv]
+    banks = (T.PB, T.PE, T.PF)
+    ready = {}
 
-    ve.tensor_tensor(T.X2[:, :], T.X4[:, own[0] * B:(own[1] + 1) * B], T.X4[:, own[0] * B:(own[1] + 1) * B],
-                     AluOpType.add).then_inc(S.ex2, 1)
-    nfw, nbw = k, nch - 1 - k
-    levels = {1: (nfw if role == 0 else nbw), 3: (nbw if role == 0 else nfw)}
-    col = 6 * B
-    off, n3 = 0, 0
-    for h in (1, 3):
-        if levels[h] >= 2:
-            te.matmul(T.PA[:, off:off + 2 * B], At(4), A(h, 2), start=True, stop=True).then_inc(S.s3, 1)
-            pa[h + 4], pa[h + 5] = col + off, col + off + B
-            off += 2 * B
-            n3 += 1
-    if max(levels.values()) >= 3:
-        te.matmul(T.PA[:, off:off + B], A(4), At(4), start=True, stop=True).then_inc(S.s3, 1)
-        pt[8] = col + off
-        off += B
-        n3 += 1
-    if n3:
-        ve.wait_ge(S.s3, n3)
-        ve.tensor_copy(T.W[:, col:col + off], T.PA[:, 0:off]).then_inc(S.e3, 1)
-        col += off
-    py, sy, ny = (T.PY0, T.PY1), (S.sY0, S.sY1), [0, 0]
+    def make_pair(i):
+        h, lv = pairs[i]
+        if lv == 1:
+            lhs, rhs = At(4), A(h, 2)
+        else:
+            te.wait_ge(S.et8, 1)
+            if lv == 3:
+                te.wait_ge(ready[(h, 1)], 1)
+            lhs, rhs = At(8), A(h + 4 * (lv - 2), 2)
+        col = (7 + 2 * i) * B
+        te.matmul(banks[i][:, 0:2 * B], lhs, rhs, start=True, stop=True).then_inc(S["sL%d" % i], 1)
+        ve.wait_ge(S["sL%d" % i], 1)
+        ve.tensor_copy(T.W[:, col:col + 2 * B], banks[i][:, 0:2 * B]).then_inc(S["eL%d" % i], 1)
+        pa[h + 4 * lv], pa[h + 4 * lv + 1] = col, col + B
+        ready[(h, lv)] = S["eL%d" % i]
+
+    for i in range(len(pairs)):
+        if pairs[i][1] < 3:
+            make_pair(i)
     for s in (0, 1):
         u = own[s]
-        for v in range(4):
-            if v != u:
-                te.matmul(py[s][:, 0:B], A(abs(u - v)), xb(v), start=(ny[s] == 0), stop=False).then_inc(sy[s], 1)
-                ny[s] += 1
-    if n3:
-        te.wait_ge(S.e3, 1)
-    off, n4 = 0, 0
-    for h in (1, 3):
-        for lv in (2, 3):
-            if levels[h] > lv:
-                te.matmul(T.PB[:, off:off + 2 * B], At(8), A(h + 4 * (lv - 2), 2), start=True, stop=True).then_inc(S.s4, 1)
-                pa[h + 4 * lv], pa[h + 4 * lv + 1] = col + off, col + off + B
-                off += 2 * B
-                n4 += 1
-    if n4:
-        ve.wait_ge(S.s4, n4)
-        ve.tensor_copy(T.W[:, col:col + off], T.PB[:, 0:off]).then_inc(S.e4, 1)
-        te.wait_ge(S.e4, 1)
+        for v in oth:
+            te.matmul(py[s][:, 0:B], A(abs(u - v)), xb(v), start=False, stop=False).then_inc(sy[s], 1)
+            ny[s] += 1
+    for i in range(len(pairs)):
+        if pairs[i][1] == 3:
+            make_pair(i)
+    ve.tensor_tensor(T.X2[:, :], xown, xown, AluOpType.add).then_inc(S.ex2, 1)
 
-    order = sorted(peer, key=lambda j: -abs(2 * j - (nch - 1)))
-    for i, j in enumerate(order):
-        land = j if j < k else j - 1
-        te.wait_ge(S["r%d" % land], per)
+    es = [j for j in others if _early(j, nch) == k][0]
+    plain_role = 1 if es < k else 0
+    part_slot = {0: slot_of(es, k), 1: nch - 1}
+    blocks = [(es, part_slot[plain_role]), (es, part_slot[1 - plain_role])]
+    whole = [j for j in others if j != es]
+    whole.sort(key=lambda j: _late_order(j, groups[j].index(peer[j]), nch).index(k))
+    blocks += [(j, slot_of(j, k)) for j in whole]
+    for i, (j, land) in enumerate(blocks):
+        h, lv = (hfw, k - 1 - j) if j < k else (hbw, j - k - 1)
+        if lv > 0:
+            te.wait_ge(ready[(h, lv)], 1)
+        te.wait_ge(S["r%d" % land], n1)
         for s in (0, 1):
             u = own[s]
             p = u + 1 + 4 * (k - 1 - j) if j < k else 4 - u + 4 * (j - k - 1)
             te.matmul(py[s][:, 0:B], A(p), T.RC[:, land * B:(land + 1) * B], start=False,
-                      stop=(i == len(order) - 1)).then_inc(sy[s], 1)
+                      stop=(i == len(blocks) - 1)).then_inc(sy[s], 1)
             ny[s] += 1
 
     ve.wait_ge(S.ex2, 1)
@@ -189,4 +242,4 @@ def rank_program(g, core, T, topo):
     g.sync.wait_ge(S.ey, 2)
     g.sync.dma_start(T.y[:, :], T.Y[:, :]).then_inc(S.st, 16)
     g.sync.wait_ge(S.st, 16)
-    g.wait_ge(S.ls, n1 + per * len(trs))
+    g.wait_ge(S.ls, nls)

from concourse.bass import DstId, RemoteDMATransfer
from concourse.mybir import AluOpType

B = 128

SCRATCH = {
    "X4": ("sbuf", [128, 4 * B], "bfloat16"),
    "X2": ("sbuf", [128, 2 * B], "bfloat16"),
    "AT": ("sbuf", [128, B], "bfloat16"),
    "W": ("sbuf", [128, 13 * B], "bfloat16"),
    "PT": ("sbuf", [128, 2 * B], "bfloat16"),
    "CD": ("sbuf", [128, 2 * B], "bfloat16"),
    "RC": ("sbuf", [128, 5 * B], "bfloat16"),
    "Y": ("sbuf", [128, 2 * B], "bfloat16"),
    "PA": ("psum", [128, 512], "float32"),
    "PB": ("psum", [128, 512], "float32"),
    "PE": ("psum", [128, 512], "float32"),
    "PF": ("psum", [128, 512], "float32"),
    "PC": ("psum", [128, 512], "float32"),
    "PD": ("psum", [128, 512], "float32"),
    "PY0": ("psum", [128, 512], "float32"),
    "PY1": ("psum", [128, 512], "float32"),
}
SEMAPHORES = ["lx", "la", "lat", "xp", "ls", "sa2", "ea2", "st2", "et2", "sa3", "ea3", "sa4", "ea4", "st8", "et8",
              "sP", "eP", "sQ", "eQ", "sL0", "sL1", "sL2", "eL0", "eL1", "eL2", "sC", "sD", "eC", "eD", "ex2",
              "sY0", "sY1", "ey", "st", "r0", "r1", "r2", "r3", "r4"]


def _early(kk, nch):
    return (kk + 1) % nch


def _late_order(kk, rr, nch):
    return [j for j in [(kk + (1 + s) * (1 - 2 * rr)) % nch for s in range(nch - 1)] if j != _early(kk, nch)]


def rank_program(g, core, T, topo):
    if T.rank_of(core) is None:
        return
    S = T.sem
    te, ve = g.tensor, g.vector

    cores = list(T.cores)
    chips = []
    for c in cores:
        if topo.chip(c) not in chips:
            chips.append(topo.chip(c))
    groups = [[c for c in cores if topo.chip(c) == ch] for ch in chips]
    nch = len(chips)
    k = chips.index(topo.chip(core))
    role = groups[k].index(core)
    partner = groups[k][1 - role]
    others = [j for j in range(nch) if j != k]
    peer = {j: [c for c in groups[j] if topo.die(c) == topo.die(core)][0] for j in others}
    m = topo.mask(core, partner)
    for j in others:
        for c in groups[j]:
            assert topo.may_write(core, c)
            m &= topo.mask(core, c)
    n1 = sum((m >> i) & 1 for i in range(m.bit_length()))

    def xb(v):
        return T.X4[:, v * B:(v + 1) * B]

    def slot_of(src_chip, dst_chip):
        return src_chip if src_chip < dst_chip else src_chip - 1

    own = (2 * role, 2 * role + 1)
    oth = (2 - 2 * role, 3 - 2 * role)
    xown = T.X4[:, own[0] * B:(own[1] + 1) * B]
    je = _early(k, nch)
    qe = 0 if je > k else 1
    squared = qe == role
    mylate = _late_order(k, role, nch)
    need_c, need_d = any(j > k for j in mylate), any(j < k for j in mylate)
    nfw, nbw = k, nch - 1 - k
    hfw, hbw = (1, 3) if role == 0 else (3, 1)
    levels = {hfw: nfw, hbw: nbw}
    need8 = max(levels.values()) >= 3

    g.sync.dma_start(xown, T.x[:, :]).then_inc(S.lx, 16)
    g.scalar.dma_start(T.W[:, 0:B], T.a[:, :]).then_inc(S.la, 16)
    g.sync.dma_start(T.AT[:, :], T.at[:, :]).then_inc(S.lat, 16)

    rid, pid, _se = topo.addr(partner)
    g.wait_ge(S.lx, 16)
    g.remote_dma(out_ap=xown, in_ap=xown, remote_sem=S.xp, local_sem=S.ls, pid=pid, routing_id=rid, dma_engine_mask=m)
    nls = n1

    pa = {1: 0, 2: B, 3: 3 * B, 4: 4 * B}
    pt = {2: 2 * B, 4: 5 * B, 8: 6 * B}

    def A(p, n=1):
        return T.W[:, pa[p]:pa[p] + n * B]

    def At(q):
        return T.W[:, pt[q]:pt[q] + B]

    te.wait_ge(S.la, 16)
    te.wait_ge(S.lat, 16)
    te.matmul(T.PA[:, 0:B], T.AT[:, :], A(1), start=True, stop=True).then_inc(S.sa2, 1)
    te.matmul(T.PB[:, 0:B], A(1), T.AT[:, :], start=True, stop=True).then_inc(S.st2, 1)
    ve.wait_ge(S.sa2, 1)
    ve.tensor_copy(A(2), T.PA[:, 0:B]).then_inc(S.ea2, 1)
    ve.wait_ge(S.st2, 1)
    ve.tensor_copy(At(2), T.PB[:, 0:B]).then_inc(S.et2, 1)
    te.wait_ge(S.ea2, 1)
    te.wait_ge(S.lx, 16)
    ve.wait_ge(S.lx, 16)
    te.matmul(T.PA[:, 0:B], A(1), xb(own[qe]), start=True, stop=True).then_inc(S.sP, 1)
    te.matmul(T.PE[:, 0:B], T.AT[:, :], A(2), start=True, stop=True).then_inc(S.sa3, 1)
    ve.wait_ge(S.sP, 1)
    ve.tensor_tensor(T.PT[:, 0:B], T.PA[:, 0:B], xb(own[1 - qe]), AluOpType.add).then_inc(S.eP, 1)
    ve.wait_ge(S.sa3, 1)
    ve.tensor_copy(A(3), T.PE[:, 0:B]).then_inc(S.ea3, 1)
    te.wait_ge(S.eP, 1)
    if squared:
        te.matmul(T.PA[:, 0:B], A(2), T.PT[:, 0:B], start=True, stop=True).then_inc(S.sQ, 1)
        ve.wait_ge(S.sQ, 1)
        ve.tensor_copy(T.PT[:, B:2 * B], T.PA[:, 0:B]).then_inc(S.eQ, 1)
    te.wait_ge(S.et2, 1)
    te.matmul(T.PF[:, 0:B], At(2), A(2), start=True, stop=True).then_inc(S.sa4, 1)
    te.matmul(T.PF[:, B:2 * B], A(2), At(2), start=True, stop=True).then_inc(S.sa4, 1)
    ve.wait_ge(S.sa4, 2)
    ve.tensor_copy(T.W[:, 4 * B:6 * B], T.PF[:, 0:2 * B]).then_inc(S.ea4, 1)

    g.wait_ge(S.eP, 1)
    if squared:
        g.wait_ge(S.eQ, 1)
    land = slot_of(k, je) if role == 0 else nch - 1
    ids = []
    for c in groups[je]:
        rid, pid, _se = topo.addr(c)
        ids.append(DstId(rid=rid, pnc=pid))
    g.remote_dma_fused([RemoteDMATransfer(dst_ids=ids, dma_engine_mask=m, remote_sem=S["r%d" % land],
                                          srcs=[T.PT[:, B:2 * B] if squared else T.PT[:, 0:B]],
                                          dsts=[T.RC[:, land * B:(land + 1) * B] for _c in ids])],
                       local_sem=S.ls)
    nls += n1

    te.wait_ge(S.ea3, 1)
    jobs = []
    if need_c:
        jobs.append((T.PC, S.sC, [(3, 0), (2, 1), (1, 2)], 3, 0, S.eC))
    if need_d:
        jobs.append((T.PD, S.sD, [(1, 1), (2, 2), (3, 3)], 0, 1, S.eD))
    jobs.sort(key=lambda jb: len([1 for (_p, v) in jb[2] if v in oth]))
    for (ps, sem, terms, _plain, _q, _done) in jobs:
        mine = [t for t in terms if t[1] in own]
        for i, (p, v) in enumerate(mine):
            te.matmul(ps[:, 0:B], A(p), xb(v), start=(i == 0), stop=False).then_inc(sem, 1)
    py, sy, ny = (T.PY0, T.PY1), (S.sY0, S.sY1), [0, 0]
    for s in (0, 1):
        te.matmul(py[s][:, 0:B], A(1), xb(own[1 - s]), start=True, stop=False).then_inc(sy[s], 1)
        ny[s] += 1

    te.wait_ge(S.xp, n1)
    ve.wait_ge(S.xp, n1)
    for (ps, sem, terms, plain, q, done) in jobs:
        theirs = [t for t in terms if t[1] in oth]
        for i, (p, v) in enumerate(theirs):
            te.matmul(ps[:, 0:B], A(p), xb(v), start=False, stop=(i == len(theirs) - 1)).then_inc(sem, 1)
        ve.wait_ge(sem, len(terms))
        ve.tensor_tensor(T.CD[:, q * B:(q + 1) * B], ps[:, 0:B], xb(plain), AluOpType.add).then_inc(done, 1)
        dests = [j for j in mylate if (j > k) == (q == 0)]
        land = k if q == 0 else k - 1
        ids = []
        for j in dests:
            rid, pid, _se = topo.addr(peer[j])
            ids.append(DstId(rid=rid, pnc=pid))
        g.wait_ge(done, 1)
        g.remote_dma_fused([RemoteDMATransfer(dst_ids=ids, dma_engine_mask=m, remote_sem=S["r%d" % land],
                                              srcs=[T.CD[:, q * B:(q + 1) * B]],
                                              dsts=[T.RC[:, land * B:(land + 1) * B] for _j in dests])],
                           local_sem=S.ls)
        nls += n1

    te.wait_ge(S.ea4, 1)
    if squared:
        te.wait_ge(S.eQ, 1)
    if need8:
        te.matmul(T.PA[:, 0:B], A(4), At(4), start=True, stop=True).then_inc(S.st8, 1)
        ve.wait_ge(S.st8, 1)
        ve.tensor_copy(At(8), T.PA[:, 0:B]).then_inc(S.et8, 1)
    pairs = [(h, lv) for lv in (1, 2, 3) for h in (1, 3) if levels[h] > lv]
    banks = (T.PB, T.PE, T.PF)
    ready = {}

    def make_pair(i):
        h, lv = pairs[i]
        if lv == 1:
            lhs, rhs = At(4), A(h, 2)
        else:
            te.wait_ge(S.et8, 1)
            if lv == 3:
                te.wait_ge(ready[(h, 1)], 1)
            lhs, rhs = At(8), A(h + 4 * (lv - 2), 2)
        col = (7 + 2 * i) * B
        te.matmul(banks[i][:, 0:2 * B], lhs, rhs, start=True, stop=True).then_inc(S["sL%d" % i], 1)
        ve.wait_ge(S["sL%d" % i], 1)
        ve.tensor_copy(T.W[:, col:col + 2 * B], banks[i][:, 0:2 * B]).then_inc(S["eL%d" % i], 1)
        pa[h + 4 * lv], pa[h + 4 * lv + 1] = col, col + B
        ready[(h, lv)] = S["eL%d" % i]

    for i in range(len(pairs)):
        if pairs[i][1] < 3:
            make_pair(i)
    for s in (0, 1):
        u = own[s]
        for v in oth:
            te.matmul(py[s][:, 0:B], A(abs(u - v)), xb(v), start=False, stop=False).then_inc(sy[s], 1)
            ny[s] += 1
    for i in range(len(pairs)):
        if pairs[i][1] == 3:
            make_pair(i)
    ve.tensor_tensor(T.X2[:, :], xown, xown, AluOpType.add).then_inc(S.ex2, 1)

    es = [j for j in others if _early(j, nch) == k][0]
    plain_role = 1 if es < k else 0
    part_slot = {0: slot_of(es, k), 1: nch - 1}
    blocks = [(es, part_slot[plain_role]), (es, part_slot[1 - plain_role])]
    whole = [j for j in others if j != es]
    whole.sort(key=lambda j: _late_order(j, groups[j].index(peer[j]), nch).index(k))
    blocks += [(j, slot_of(j, k)) for j in whole]
    for i, (j, land) in enumerate(blocks):
        h, lv = (hfw, k - 1 - j) if j < k else (hbw, j - k - 1)
        if lv > 0:
            te.wait_ge(ready[(h, lv)], 1)
        te.wait_ge(S["r%d" % land], n1)
        for s in (0, 1):
            u = own[s]
            p = u + 1 + 4 * (k - 1 - j) if j < k else 4 - u + 4 * (j - k - 1)
            te.matmul(py[s][:, 0:B], A(p), T.RC[:, land * B:(land + 1) * B], start=False,
                      stop=(i == len(blocks) - 1)).then_inc(sy[s], 1)
            ny[s] += 1

    ve.wait_ge(S.ex2, 1)
    for s in (0, 1):
        ve.wait_ge(sy[s], ny[s])
        ve.tensor_tensor(T.Y[:, s * B:(s + 1) * B], py[s][:, 0:B], T.X2[:, s * B:(s + 1) * B],
                         AluOpType.add).then_inc(S.ey, 1)
    g.sync.wait_ge(S.ey, 2)
    g.sync.dma_start(T.y[:, :], T.Y[:, :]).then_inc(S.st, 16)
    g.sync.wait_ge(S.st, 16)
    g.wait_ge(S.ls, nls)
